import numpy as np
import ml_dtypes

BF16 = ml_dtypes.bfloat16


def bf(x):
    return np.asarray(x, np.float32).astype(BF16)


def f32(x):
    return np.asarray(x, np.float32)


def f64(x):
    return np.asarray(x).astype(np.float64)


def striped(idx):
    return np.tile(idx.reshape(-1, 16).T, (8, 1))


S, K, M, N = 256, 128, 512, 256


def setup_inputs():
    return {"table": bf(np.random.standard_normal((K, S))), "w": bf(np.random.standard_normal((K, M)) / np.sqrt(K)), "offs": striped(np.random.permutation(S))}


def reference(table, w, offs):
    idx = offs[:16].T.reshape(-1)
    x = f64(table)[:, idx]
    y = f64(w).T @ x
    return y

@@ -1,0 +1,42 @@
+import concourse.mybir as mybir
+
+BF16, F32, U16 = mybir.dt.bfloat16, mybir.dt.float32, mybir.dt.uint16
+
+P = 128
+S = 256
+M = 512
+N = 256
+
+FLOPS = 2 * P * M * N
+
+
+def tile_gather_matmul_kernel(tc, table, w, offs, out):
+    nc = tc.nc
+    with (
+        tc.tile_pool(name="held", bufs=1) as held,
+        tc.tile_pool(name="staging", bufs=M // P) as staging,
+        tc.psum_pool(name="banks", bufs=M // P) as banks,
+    ):
+        offsets = held.tile([P, N // 16], U16, name="offsets")
+        nc.sync.dma_start(offsets[:], offs)
+        tokens = held.tile([P, S], BF16, name="tokens")
+        nc.scalar.dma_start(tokens[:], table)
+        weights = held.tile([P, M], BF16, name="weights")
+        nc.sync.dma_start(weights[:], w)
+
+        for block in range(M // P):
+            bank = banks.tile([P, N], F32, name="bank")
+            nc.tensor.matmul(
+                bank[:],
+                weights[:, block * P : (block + 1) * P],
+                tokens[:].indirect(offsets[:]),
+                start=True,
+                stop=True,
+            )
+            rows = staging.tile([P, N], F32, name="rows")
+            if block % 2 == 0:
+                nc.vector.tensor_copy(rows[:], bank[:])
+                nc.sync.dma_start(out[block * P : (block + 1) * P, :], rows[:])
+            else:
+                nc.scalar.copy(rows[:], bank[:])
+                nc.scalar.dma_start(out[block * P : (block + 1) * P, :], rows[:])

@@ -6,16 +6,20 @@ P = 128
 S = 256
 M = 512
 N = 256
+BLOCKS = M // P
 
 FLOPS = 2 * P * M * N
+
+WARMUPS = 16
 
 
 def tile_gather_matmul_kernel(tc, table, w, offs, out):
     nc = tc.nc
     with (
         tc.tile_pool(name="held", bufs=1) as held,
-        tc.tile_pool(name="staging", bufs=M // P) as staging,
-        tc.psum_pool(name="banks", bufs=M // P) as banks,
+        tc.tile_pool(name="staging", bufs=BLOCKS) as staging,
+        tc.psum_pool(name="banks", bufs=BLOCKS) as banks,
+        tc.psum_pool(name="idle", bufs=1) as idle,
     ):
         offsets = held.tile([P, N // 16], U16, name="offsets")
         nc.sync.dma_start(offsets[:], offs)
@@ -24,7 +28,13 @@ def tile_gather_matmul_kernel(tc, table, w, offs, out):
         weights = held.tile([P, M], BF16, name="weights")
         nc.sync.dma_start(weights[:], w)
 
-        for block in range(M // P):
+        zeros = held.tile([P, P], BF16, name="zeros")
+        nc.vector.memset(zeros[:], 0.0)
+        unread = idle.tile([P, P], F32, name="unread")
+        for turn in range(WARMUPS):
+            nc.tensor.matmul(unread[:], zeros[:], zeros[:], start=True, stop=True)
+
+        for block in range(BLOCKS):
             bank = banks.tile([P, N], F32, name="bank")
             nc.tensor.matmul(
                 bank[:],

@@ -25,8 +25,9 @@ def tile_gather_matmul_kernel(tc, table, w, offs, out):
         nc.sync.dma_start(offsets[:], offs)
         tokens = held.tile([P, S], BF16, name="tokens")
         nc.scalar.dma_start(tokens[:], table)
-        weights = held.tile([P, M], BF16, name="weights")
-        nc.sync.dma_start(weights[:], w)
+        weights = [held.tile([P, M // 2], BF16, name="weights%d" % half) for half in range(2)]
+        nc.sync.dma_start(weights[0][:], w[:, : M // 2])
+        nc.scalar.dma_start(weights[1][:], w[:, M // 2 :])
 
         zeros = held.tile([P, P], BF16, name="zeros")
         nc.vector.memset(zeros[:], 0.0)
@@ -38,7 +39,7 @@ def tile_gather_matmul_kernel(tc, table, w, offs, out):
             bank = banks.tile([P, N], F32, name="bank")
             nc.tensor.matmul(
                 bank[:],
-                weights[:, block * P : (block + 1) * P],
+                weights[block // 2][:, (block % 2) * P : (block % 2 + 1) * P],
                 tokens[:].indirect(offsets[:]),
                 start=True,
                 stop=True,

@@ -10,8 +10,6 @@ BLOCKS = M // P
 
 FLOPS = 2 * P * M * N
 
-WARMUPS = 16
-
 
 def tile_gather_matmul_kernel(tc, table, w, offs, out):
     nc = tc.nc
@@ -19,7 +17,6 @@ def tile_gather_matmul_kernel(tc, table, w, offs, out):
         tc.tile_pool(name="held", bufs=1) as held,
         tc.tile_pool(name="staging", bufs=BLOCKS) as staging,
         tc.psum_pool(name="banks", bufs=BLOCKS) as banks,
-        tc.psum_pool(name="idle", bufs=1) as idle,
     ):
         offsets = held.tile([P, N // 16], U16, name="offsets")
         nc.sync.dma_start(offsets[:], offs)
@@ -28,12 +25,6 @@ def tile_gather_matmul_kernel(tc, table, w, offs, out):
         weights = [held.tile([P, M // 2], BF16, name="weights%d" % half) for half in range(2)]
         nc.sync.dma_start(weights[0][:], w[:, : M // 2])
         nc.scalar.dma_start(weights[1][:], w[:, M // 2 :])
-
-        zeros = held.tile([P, P], BF16, name="zeros")
-        nc.vector.memset(zeros[:], 0.0)
-        unread = idle.tile([P, P], F32, name="unread")
-        for turn in range(WARMUPS):
-            nc.tensor.matmul(unread[:], zeros[:], zeros[:], start=True, stop=True)
 
         for block in range(BLOCKS):
             bank = banks.tile([P, N], F32, name="bank")

@@ -18,12 +18,12 @@ def tile_gather_matmul_kernel(tc, table, w, offs, out):
         tc.tile_pool(name="staging", bufs=BLOCKS) as staging,
         tc.psum_pool(name="banks", bufs=BLOCKS) as banks,
     ):
-        offsets = held.tile([P, N // 16], U16, name="offsets")
-        nc.sync.dma_start(offsets[:], offs)
-        tokens = held.tile([P, S], BF16, name="tokens")
-        nc.scalar.dma_start(tokens[:], table)
         weights = [held.tile([P, M // 2], BF16, name="weights%d" % half) for half in range(2)]
         nc.sync.dma_start(weights[0][:], w[:, : M // 2])
+        tokens = held.tile([P, S], BF16, name="tokens")
+        nc.scalar.dma_start(tokens[:], table)
+        offsets = held.tile([P, N // 16], U16, name="offsets")
+        nc.sync.dma_start(offsets[:], offs)
         nc.scalar.dma_start(weights[1][:], w[:, M // 2 :])
 
         for block in range(BLOCKS):

@@ -35,7 +35,7 @@ def tile_gather_matmul_kernel(tc, table, w, offs, out):
                 start=True,
                 stop=True,
             )
-            rows = staging.tile([P, N], F32, name="rows")
+            rows = staging.tile([P, N], F32, name="rows", align_bytes=4 * N)
             if block % 2 == 0:
                 nc.vector.tensor_copy(rows[:], bank[:])
                 nc.sync.dma_start(out[block * P : (block + 1) * P, :], rows[:])

@@ -18,9 +18,9 @@ def tile_gather_matmul_kernel(tc, table, w, offs, out):
         tc.tile_pool(name="staging", bufs=BLOCKS) as staging,
         tc.psum_pool(name="banks", bufs=BLOCKS) as banks,
     ):
-        weights = [held.tile([P, M // 2], BF16, name="weights%d" % half) for half in range(2)]
+        weights = [held.tile([P, M // 2], BF16, name="weights%d" % half, align_bytes=M) for half in range(2)]
         nc.sync.dma_start(weights[0][:], w[:, : M // 2])
-        tokens = held.tile([P, S], BF16, name="tokens")
+        tokens = held.tile([P, S], BF16, name="tokens", align_bytes=2 * S)
         nc.scalar.dma_start(tokens[:], table)
         offsets = held.tile([P, N // 16], U16, name="offsets")
         nc.sync.dma_start(offsets[:], offs)

import concourse.mybir as mybir

BF16, F32, U16 = mybir.dt.bfloat16, mybir.dt.float32, mybir.dt.uint16

P = 128
S = 256
M = 512
N = 256
BLOCKS = M // P

FLOPS = 2 * P * M * N


def tile_gather_matmul_kernel(tc, table, w, offs, out):
    nc = tc.nc
    with (
        tc.tile_pool(name="held", bufs=1) as held,
        tc.tile_pool(name="staging", bufs=BLOCKS) as staging,
        tc.psum_pool(name="banks", bufs=BLOCKS) as banks,
    ):
        weights = [held.tile([P, M // 2], BF16, name="weights%d" % half, align_bytes=M) for half in range(2)]
        nc.sync.dma_start(weights[0][:], w[:, : M // 2])
        tokens = held.tile([P, S], BF16, name="tokens", align_bytes=2 * S)
        nc.scalar.dma_start(tokens[:], table)
        offsets = held.tile([P, N // 16], U16, name="offsets")
        nc.sync.dma_start(offsets[:], offs)
        nc.scalar.dma_start(weights[1][:], w[:, M // 2 :])

        for block in range(BLOCKS):
            bank = banks.tile([P, N], F32, name="bank")
            nc.tensor.matmul(
                bank[:],
                weights[block // 2][:, (block % 2) * P : (block % 2 + 1) * P],
                tokens[:].indirect(offsets[:]),
                start=True,
                stop=True,
            )
            rows = staging.tile([P, N], F32, name="rows", align_bytes=4 * N)
            if block % 2 == 0:
                nc.vector.tensor_copy(rows[:], bank[:])
                nc.sync.dma_start(out[block * P : (block + 1) * P, :], rows[:])
            else:
                nc.scalar.copy(rows[:], bank[:])
                nc.scalar.dma_start(out[block * P : (block + 1) * P, :], rows[:])
